import numpy as np
import ml_dtypes


def mxq(x, axis, fmt="e4m3"):
    dtype, down = {"e4m3": (ml_dtypes.float8_e4m3fn, 7), "e5m2": (ml_dtypes.float8_e5m2, 14)}[fmt]
    v = np.moveaxis(np.asarray(x, np.float32).astype(ml_dtypes.bfloat16).astype(np.float64), axis, -1)
    blocks = v.reshape(v.shape[:-1] + (-1, 32))
    amax = np.abs(blocks).max(-1, keepdims=True)
    byte = np.maximum(np.where(amax > 0, np.frexp(amax)[1] - 1 + 127, 0) - down, 1)
    scale = np.exp2(byte - 127.0)
    codes = (blocks / scale).astype(np.float32).astype(dtype).astype(np.float64)
    return np.moveaxis((codes * scale).reshape(v.shape), -1, axis)


WIDE = False


def mx_kscale(k):
    if not WIDE:
        return np.ones(k)
    levels = np.array([10, -10, 5, -5, 0])
    if k % 512:
        return np.exp2(np.random.permutation(np.resize(levels, k // 32))).repeat(32)
    a = np.empty((k // 512, 16))
    for p in range(k // 512):
        a[p, :8] = np.random.permutation(np.resize(levels, 8))
        for g in range(8):
            far = levels[np.abs(levels - a[p, g]) >= 10]
            a[p, g + 8] = far[np.random.randint(len(far))]
    return np.exp2(a.ravel()).repeat(32)


def f64(x):
    return np.asarray(x).astype(np.float64)


def striped(idx):
    return np.tile(idx.reshape(-1, 16).T, (8, 1)).astype(np.uint16)


def unstriped(offs):
    return offs[:16].T.reshape(-1).astype(np.int64)


def gelu(v):
    return 0.5 * v * (1.0 + np.tanh(np.sqrt(2.0 / np.pi) * (v + 0.044715 * v**3)))


K, T, D, S, V, H, N = 512, 4096, 4, 1024, 256, 512, 256


def setup_inputs():
    n = np.random.standard_normal
    s = mx_kscale(K)[:, None]
    u = mx_kscale(H)
    return {
        "xT": (n((K, T)) * s).astype(np.float32),
        "w1": (n((K, H)) / np.sqrt(K) / s * u).astype(np.float32),
        "w2": (n((H, N)) / np.sqrt(H) / u[:, None]).astype(np.float32),
        "gate": np.tile(np.random.uniform(0.5, 1.5, V), (N, 1)).astype(np.float32),
        "offs": striped(np.random.permutation(T)[:S]),
        "pos1": striped(np.random.permutation(2 * V)[:V]),
    }


def reference(xT, w1, w2, gate, offs, pos1):
    h = gelu(mxq(f64(w1), 0, "e4m3").T @ mxq(f64(xT)[:, unstriped(offs)], 0, "e4m3"))
    z = h.reshape(H, V, D).max(axis=2)
    out = np.zeros((N, 2 * V))
    out[:, unstriped(pos1)] = f64(gate) * (mxq(f64(w2), 0, "e4m3").T @ mxq(z, 0, "e4m3"))
    return out

@@ -1,0 +1,165 @@
+from contextlib import ExitStack
+
+import concourse.mybir as mybir
+
+K, T, S, V, H, N = 512, 4096, 1024, 256, 512, 256
+D = S // V
+FLOPS = 2 * K * S * H + 2 * H * V * N
+
+F32 = mybir.dt.float32
+BF16 = mybir.dt.bfloat16
+U32 = mybir.dt.uint32
+U16 = mybir.dt.uint16
+U8 = mybir.dt.uint8
+FP8X4 = mybir.dt.float8_e4m3fn_x4
+GELU = mybir.ActivationFunctionType.Gelu_apprx_tanh
+MAX = mybir.AluOpType.max
+MULT = mybir.AluOpType.mult
+
+P = 128
+PACK = 4
+SLICE = 512
+CHUNK = 128
+PIECE = 256
+GROUPS = PIECE // D
+
+
+def tile_picked_vpool_gelu_e_kernel(tc, xT, w1, w2, gate, offs, pos1, out):
+    nc = tc.nc
+    with ExitStack() as ctx:
+        keep = ctx.enter_context(tc.tile_pool(name="keep", bufs=1))
+        hbanks = ctx.enter_context(tc.psum_pool(name="hbanks", bufs=6))
+        obanks = ctx.enter_context(tc.psum_pool(name="obanks", bufs=2))
+
+        offsets = keep.tile([P, S // 16], U16, name="offsets")
+        places = keep.tile([P, V // 16], U16, name="places")
+        nc.sync.dma_start(offsets[:], offs)
+        planes = [keep.tile([P, T], F32, name=f"plane{j}") for j in range(PACK)]
+        w1_raw = keep.tile([P, PACK, H], F32, name="w1_raw")
+        w2_raw = keep.tile([P, PACK, N], F32, name="w2_raw")
+        gates = keep.tile([P, N // P, V], F32, name="gates")
+        x_rows = xT.rearrange("(p j) w -> p j w", j=PACK)
+        for j in range(PACK):
+            if j == PACK - 1:
+                nc.sync.dma_start(out=w1_raw[:], in_=w1.rearrange("(p j) w -> p j w", j=PACK))
+            nc.sync.dma_start(out=planes[j][:], in_=x_rows[:, j, :])
+        nc.sync.dma_start(out=w2_raw[:], in_=w2.rearrange("(p j) w -> p j w", j=PACK))
+        nc.sync.dma_start(places[:], pos1)
+        nc.sync.dma_start(out=gates[:], in_=gate.rearrange("(o p) v -> p o v", p=P))
+
+        windows = [keep.tile([P, 2 * V], F32, name=f"window{o}") for o in range(N // P)]
+        for window in windows:
+            nc.vector.memset(window[:], 0.0)
+        warm_in = keep.tile([P, 1], F32, name="warm_in")
+        warm_out = keep.tile([P, 1], F32, name="warm_out")
+        nc.vector.memset(warm_in[:], 0.0)
+        nc.scalar.activation(warm_out[:], warm_in[:], GELU)
+
+        w1_grouped = keep.tile([P, H * PACK], BF16, name="w1_grouped", align_bytes=64)
+        w1_codes = keep.tile([P, H], U32, name="w1_codes", align_bytes=64)
+        w1_scales = keep.tile([P, H], U8, name="w1_scales", align_bytes=64)
+        w2_grouped = keep.tile([P, N * PACK], BF16, name="w2_grouped", align_bytes=64)
+        w2_codes = keep.tile([P, N], U32, name="w2_codes", align_bytes=64)
+        w2_scales = keep.tile([P, N], U8, name="w2_scales", align_bytes=64)
+        x_grouped = [keep.tile([P, SLICE, PACK], BF16, name=f"x_grouped{s}", align_bytes=64) for s in range(2)]
+        x_codes = [keep.tile([P, SLICE], U32, name=f"x_codes{s}", align_bytes=64) for s in range(2)]
+        x_scales = [keep.tile([P, SLICE], U8, name=f"x_scales{s}", align_bytes=64) for s in range(2)]
+
+        def gather(j, s):
+            nc.vector.tensor_copy(
+                x_grouped[s][:, :, j], planes[j][:].indirect(offsets[:, s * (SLICE // 16) : (s + 1) * (SLICE // 16)])
+            )
+
+        def quantize_x(s):
+            nc.vector.quantize_mx(
+                out=x_codes[s][:].bitcast(FP8X4), scales=x_scales[s][:], in_=x_grouped[s][:].rearrange("p n j -> p (n j)")
+            )
+
+        for j in range(PACK - 1):
+            for s in range(2):
+                gather(j, s)
+
+        nc.scalar.copy(
+            w1_grouped[:].rearrange("p (t m j) -> p m t j", t=PACK, j=PACK), w1_raw[:].rearrange("p j (m t) -> p m t j", t=PACK)
+        )
+        nc.vector.quantize_mx(out=w1_codes[:].bitcast(FP8X4), scales=w1_scales[:], in_=w1_grouped[:])
+        nc.scalar.copy(w2_grouped[:].rearrange("p (n j) -> p n j", j=PACK), w2_raw[:].rearrange("p j n -> p n j"))
+
+        gather(PACK - 1, 0)
+        quantize_x(0)
+        gather(PACK - 1, 1)
+        quantize_x(1)
+        nc.vector.quantize_mx(out=w2_codes[:].bitcast(FP8X4), scales=w2_scales[:], in_=w2_grouped[:])
+
+        pieces = S // PIECE
+        h = [keep.tile([P, D, PIECE // CHUNK, CHUNK], BF16, name=f"h{i}", align_bytes=64) for i in range(pieces)]
+        z_codes = [keep.tile([P, GROUPS], U32, name=f"z_codes{i}", align_bytes=64) for i in range(pieces)]
+        z_scales = [keep.tile([P, GROUPS], U8, name=f"z_scales{i}", align_bytes=64) for i in range(pieces)]
+
+        def first_layer(i):
+            for c in range(PIECE // CHUNK):
+                token = i * PIECE + c * CHUNK
+                s = token // SLICE
+                cols = slice(token % SLICE, token % SLICE + CHUNK)
+                bank = hbanks.tile([P, PACK, CHUNK], F32, name="bank")
+                for t in range(PACK):
+                    nc.tensor.matmul_mx(
+                        out=bank[:, t, :],
+                        lhsT=w1_codes[:, t * P : (t + 1) * P].bitcast(FP8X4),
+                        lhsT_scale=w1_scales[:, t * P : (t + 1) * P],
+                        rhs=x_codes[s][:, cols].bitcast(FP8X4),
+                        rhs_scale=x_scales[s][:, cols],
+                        start=True,
+                        stop=True,
+                    )
+                nc.scalar.activation(
+                    h[i][:, :, c, :].rearrange("p d (v t) -> p d v t", t=PACK),
+                    bank[:].rearrange("p t (v d) -> p d v t", d=D),
+                    GELU,
+                )
+
+        def pool(i):
+            half = keep.tile([P, 2, PIECE], BF16, name=f"half{i}", align_bytes=64)
+            nc.vector.tensor_tensor(
+                half[:], h[i][:, 0:2].rearrange("p d c w -> p d (c w)"), h[i][:, 2:4].rearrange("p d c w -> p d (c w)"), MAX
+            )
+            z = keep.tile([P, GROUPS * PACK], BF16, name=f"z{i}", align_bytes=64)
+            nc.vector.tensor_tensor(z[:], half[:, 0, :], half[:, 1, :], MAX)
+            nc.vector.quantize_mx(out=z_codes[i][:].bitcast(FP8X4), scales=z_scales[i][:], in_=z[:])
+
+        def second_layer(i):
+            pair = obanks.tile([P, N // P, GROUPS], F32, name="pair")
+            for o in range(N // P):
+                nc.tensor.matmul_mx(
+                    out=pair[:, o, :],
+                    lhsT=w2_codes[:, o * P : (o + 1) * P].bitcast(FP8X4),
+                    lhsT_scale=w2_scales[:, o * P : (o + 1) * P],
+                    rhs=z_codes[i][:].bitcast(FP8X4),
+                    rhs_scale=z_scales[i][:],
+                    start=True,
+                    stop=True,
+                )
+            result = keep.tile([P, N // P, GROUPS], F32, name=f"result{i}")
+            nc.scalar.copy(result[:], pair[:])
+            for o in range(N // P):
+                nc.vector.tensor_tensor(
+                    windows[o][:].indirect(places[:, i * (GROUPS // 16) : (i + 1) * (GROUPS // 16)]),
+                    result[:, o, :],
+                    gates[:, o, i * GROUPS : (i + 1) * GROUPS],
+                    MULT,
+                )
+
+        first_layer(0)
+        first_layer(1)
+        pool(0)
+        first_layer(2)
+        pool(1)
+        second_layer(0)
+        first_layer(3)
+        pool(2)
+        second_layer(1)
+        pool(3)
+        second_layer(2)
+        second_layer(3)
+        for o in range(N // P):
+            nc.sync.dma_start(out=out[o * P : (o + 1) * P, :], in_=windows[o][:])

@@ -33,16 +33,19 @@ def tile_picked_vpool_gelu_e_kernel(tc, xT, w1, w2, gate, offs, pos1, out):
 
         offsets = keep.tile([P, S // 16], U16, name="offsets")
         places = keep.tile([P, V // 16], U16, name="places")
-        nc.sync.dma_start(offsets[:], offs)
         planes = [keep.tile([P, T], F32, name=f"plane{j}") for j in range(PACK)]
-        w1_raw = keep.tile([P, PACK, H], F32, name="w1_raw")
+        w1_raw = [keep.tile([P, PACK, H // 2], F32, name=f"w1_raw{i}") for i in range(2)]
         w2_raw = keep.tile([P, PACK, N], F32, name="w2_raw")
         gates = keep.tile([P, N // P, V], F32, name="gates")
         x_rows = xT.rearrange("(p j) w -> p j w", j=PACK)
-        for j in range(PACK):
-            if j == PACK - 1:
-                nc.sync.dma_start(out=w1_raw[:], in_=w1.rearrange("(p j) w -> p j w", j=PACK))
-            nc.sync.dma_start(out=planes[j][:], in_=x_rows[:, j, :])
+        w1_rows = w1.rearrange("(p j) w -> p j w", j=PACK)
+        nc.sync.dma_start(out=planes[0][:], in_=x_rows[:, 0, :])
+        nc.sync.dma_start(offsets[:], offs)
+        nc.sync.dma_start(out=planes[1][:], in_=x_rows[:, 1, :])
+        nc.sync.dma_start(out=planes[2][:], in_=x_rows[:, 2, :])
+        nc.sync.dma_start(out=planes[3][:], in_=x_rows[:, 3, :])
+        nc.sync.dma_start(out=w1_raw[0][:], in_=w1_rows[:, :, 0 : H // 2])
+        nc.sync.dma_start(out=w1_raw[1][:], in_=w1_rows[:, :, H // 2 : H])
         nc.sync.dma_start(out=w2_raw[:], in_=w2.rearrange("(p j) w -> p j w", j=PACK))
         nc.sync.dma_start(places[:], pos1)
         nc.sync.dma_start(out=gates[:], in_=gate.rearrange("(o p) v -> p o v", p=P))
@@ -79,32 +82,37 @@ def tile_picked_vpool_gelu_e_kernel(tc, xT, w1, w2, gate, offs, pos1, out):
             for s in range(2):
                 gather(j, s)
 
-        nc.scalar.copy(
-            w1_grouped[:].rearrange("p (t m j) -> p m t j", t=PACK, j=PACK), w1_raw[:].rearrange("p j (m t) -> p m t j", t=PACK)
-        )
-        nc.vector.quantize_mx(out=w1_codes[:].bitcast(FP8X4), scales=w1_scales[:], in_=w1_grouped[:])
+        w1_view = w1_grouped[:].rearrange("p (t m j) -> p m t j", t=PACK, j=PACK)
+        for i in range(2):
+            nc.scalar.copy(w1_view[:, i * 64 : (i + 1) * 64], w1_raw[i][:].rearrange("p j (m t) -> p m t j", t=PACK))
         nc.scalar.copy(w2_grouped[:].rearrange("p (n j) -> p n j", j=PACK), w2_raw[:].rearrange("p j n -> p n j"))
 
         gather(PACK - 1, 0)
         quantize_x(0)
         gather(PACK - 1, 1)
+        for i in range(2):
+            cols = slice(i * (H // 2), (i + 1) * (H // 2))
+            nc.vector.quantize_mx(
+                out=w1_codes[:, cols].bitcast(FP8X4), scales=w1_scales[:, cols], in_=w1_grouped[:, i * 1024 : (i + 1) * 1024]
+            )
         quantize_x(1)
         nc.vector.quantize_mx(out=w2_codes[:].bitcast(FP8X4), scales=w2_scales[:], in_=w2_grouped[:])
 
         pieces = S // PIECE
-        h = [keep.tile([P, D, PIECE // CHUNK, CHUNK], BF16, name=f"h{i}", align_bytes=64) for i in range(pieces)]
+        h = [keep.tile([P, 2, D, GROUPS * 2], BF16, name=f"h{i}", align_bytes=64) for i in range(pieces)]
         z_codes = [keep.tile([P, GROUPS], U32, name=f"z_codes{i}", align_bytes=64) for i in range(pieces)]
         z_scales = [keep.tile([P, GROUPS], U8, name=f"z_scales{i}", align_bytes=64) for i in range(pieces)]
 
         def first_layer(i):
-            for c in range(PIECE // CHUNK):
-                token = i * PIECE + c * CHUNK
-                s = token // SLICE
-                cols = slice(token % SLICE, token % SLICE + CHUNK)
-                bank = hbanks.tile([P, PACK, CHUNK], F32, name="bank")
-                for t in range(PACK):
+            token = i * PIECE
+            s = token // SLICE
+            cols = slice(token % SLICE, token % SLICE + PIECE)
+            for a in range(2):
+                bank = hbanks.tile([P, 2, PIECE], F32, name="bank")
+                for b in range(2):
+                    t = 2 * a + b
                     nc.tensor.matmul_mx(
-                        out=bank[:, t, :],
+                        out=bank[:, b, :],
                         lhsT=w1_codes[:, t * P : (t + 1) * P].bitcast(FP8X4),
                         lhsT_scale=w1_scales[:, t * P : (t + 1) * P],
                         rhs=x_codes[s][:, cols].bitcast(FP8X4),
@@ -113,19 +121,27 @@ def tile_picked_vpool_gelu_e_kernel(tc, xT, w1, w2, gate, offs, pos1, out):
                         stop=True,
                     )
                 nc.scalar.activation(
-                    h[i][:, :, c, :].rearrange("p d (v t) -> p d v t", t=PACK),
-                    bank[:].rearrange("p t (v d) -> p d v t", d=D),
+                    h[i][:, a].rearrange("p d (v b) -> p d v b", b=2),
+                    bank[:].rearrange("p b (v d) -> p d v b", d=D),
                     GELU,
                 )
 
         def pool(i):
-            half = keep.tile([P, 2, PIECE], BF16, name=f"half{i}", align_bytes=64)
+            half = keep.tile([P, 2, 2, GROUPS * 2], BF16, name=f"half{i}", align_bytes=64)
             nc.vector.tensor_tensor(
-                half[:], h[i][:, 0:2].rearrange("p d c w -> p d (c w)"), h[i][:, 2:4].rearrange("p d c w -> p d (c w)"), MAX
+                half[:].rearrange("p a d w -> p a (d w)"),
+                h[i][:, :, 0:2].rearrange("p a d w -> p a (d w)"),
+                h[i][:, :, 2:4].rearrange("p a d w -> p a (d w)"),
+                MAX,
             )
-            z = keep.tile([P, GROUPS * PACK], BF16, name=f"z{i}", align_bytes=64)
-            nc.vector.tensor_tensor(z[:], half[:, 0, :], half[:, 1, :], MAX)
-            nc.vector.quantize_mx(out=z_codes[i][:].bitcast(FP8X4), scales=z_scales[i][:], in_=z[:])
+            z = keep.tile([P, GROUPS, 2, 2], BF16, name=f"z{i}", align_bytes=64)
+            nc.vector.tensor_tensor(
+                z[:],
+                half[:, :, 0].rearrange("p a (v b) -> p v a b", b=2),
+                half[:, :, 1].rearrange("p a (v b) -> p v a b", b=2),
+                MAX,
+            )
+            nc.vector.quantize_mx(out=z_codes[i][:].bitcast(FP8X4), scales=z_scales[i][:], in_=z[:].rearrange("p v a b -> p (v a b)"))
 
         def second_layer(i):
             pair = obanks.tile([P, N // P, GROUPS], F32, name="pair")

from contextlib import ExitStack

import concourse.mybir as mybir

K, T, S, V, H, N = 512, 4096, 1024, 256, 512, 256
D = S // V
FLOPS = 2 * K * S * H + 2 * H * V * N

F32 = mybir.dt.float32
BF16 = mybir.dt.bfloat16
U32 = mybir.dt.uint32
U16 = mybir.dt.uint16
U8 = mybir.dt.uint8
FP8X4 = mybir.dt.float8_e4m3fn_x4
GELU = mybir.ActivationFunctionType.Gelu_apprx_tanh
MAX = mybir.AluOpType.max
MULT = mybir.AluOpType.mult

P = 128
PACK = 4
SLICE = 512
CHUNK = 128
PIECE = 256
GROUPS = PIECE // D


def tile_picked_vpool_gelu_e_kernel(tc, xT, w1, w2, gate, offs, pos1, out):
    nc = tc.nc
    with ExitStack() as ctx:
        keep = ctx.enter_context(tc.tile_pool(name="keep", bufs=1))
        hbanks = ctx.enter_context(tc.psum_pool(name="hbanks", bufs=6))
        obanks = ctx.enter_context(tc.psum_pool(name="obanks", bufs=2))

        offsets = keep.tile([P, S // 16], U16, name="offsets")
        places = keep.tile([P, V // 16], U16, name="places")
        planes = [keep.tile([P, T], F32, name=f"plane{j}") for j in range(PACK)]
        w1_raw = [keep.tile([P, PACK, H // 2], F32, name=f"w1_raw{i}") for i in range(2)]
        w2_raw = keep.tile([P, PACK, N], F32, name="w2_raw")
        gates = keep.tile([P, N // P, V], F32, name="gates")
        x_rows = xT.rearrange("(p j) w -> p j w", j=PACK)
        w1_rows = w1.rearrange("(p j) w -> p j w", j=PACK)
        nc.sync.dma_start(out=planes[0][:], in_=x_rows[:, 0, :])
        nc.sync.dma_start(offsets[:], offs)
        nc.sync.dma_start(out=planes[1][:], in_=x_rows[:, 1, :])
        nc.sync.dma_start(out=planes[2][:], in_=x_rows[:, 2, :])
        nc.sync.dma_start(out=planes[3][:], in_=x_rows[:, 3, :])
        nc.sync.dma_start(out=w1_raw[0][:], in_=w1_rows[:, :, 0 : H // 2])
        nc.sync.dma_start(out=w1_raw[1][:], in_=w1_rows[:, :, H // 2 : H])
        nc.sync.dma_start(out=w2_raw[:], in_=w2.rearrange("(p j) w -> p j w", j=PACK))
        nc.sync.dma_start(places[:], pos1)
        nc.sync.dma_start(out=gates[:], in_=gate.rearrange("(o p) v -> p o v", p=P))

        windows = [keep.tile([P, 2 * V], F32, name=f"window{o}") for o in range(N // P)]
        for window in windows:
            nc.vector.memset(window[:], 0.0)
        warm_in = keep.tile([P, 1], F32, name="warm_in")
        warm_out = keep.tile([P, 1], F32, name="warm_out")
        nc.vector.memset(warm_in[:], 0.0)
        nc.scalar.activation(warm_out[:], warm_in[:], GELU)

        w1_grouped = keep.tile([P, H * PACK], BF16, name="w1_grouped", align_bytes=64)
        w1_codes = keep.tile([P, H], U32, name="w1_codes", align_bytes=64)
        w1_scales = keep.tile([P, H], U8, name="w1_scales", align_bytes=64)
        w2_grouped = keep.tile([P, N * PACK], BF16, name="w2_grouped", align_bytes=64)
        w2_codes = keep.tile([P, N], U32, name="w2_codes", align_bytes=64)
        w2_scales = keep.tile([P, N], U8, name="w2_scales", align_bytes=64)
        x_grouped = [keep.tile([P, SLICE, PACK], BF16, name=f"x_grouped{s}", align_bytes=64) for s in range(2)]
        x_codes = [keep.tile([P, SLICE], U32, name=f"x_codes{s}", align_bytes=64) for s in range(2)]
        x_scales = [keep.tile([P, SLICE], U8, name=f"x_scales{s}", align_bytes=64) for s in range(2)]

        def gather(j, s):
            nc.vector.tensor_copy(
                x_grouped[s][:, :, j], planes[j][:].indirect(offsets[:, s * (SLICE // 16) : (s + 1) * (SLICE // 16)])
            )

        def quantize_x(s):
            nc.vector.quantize_mx(
                out=x_codes[s][:].bitcast(FP8X4), scales=x_scales[s][:], in_=x_grouped[s][:].rearrange("p n j -> p (n j)")
            )

        for j in range(PACK - 1):
            for s in range(2):
                gather(j, s)

        w1_view = w1_grouped[:].rearrange("p (t m j) -> p m t j", t=PACK, j=PACK)
        for i in range(2):
            nc.scalar.copy(w1_view[:, i * 64 : (i + 1) * 64], w1_raw[i][:].rearrange("p j (m t) -> p m t j", t=PACK))
        nc.scalar.copy(w2_grouped[:].rearrange("p (n j) -> p n j", j=PACK), w2_raw[:].rearrange("p j n -> p n j"))

        gather(PACK - 1, 0)
        quantize_x(0)
        gather(PACK - 1, 1)
        for i in range(2):
            cols = slice(i * (H // 2), (i + 1) * (H // 2))
            nc.vector.quantize_mx(
                out=w1_codes[:, cols].bitcast(FP8X4), scales=w1_scales[:, cols], in_=w1_grouped[:, i * 1024 : (i + 1) * 1024]
            )
        quantize_x(1)
        nc.vector.quantize_mx(out=w2_codes[:].bitcast(FP8X4), scales=w2_scales[:], in_=w2_grouped[:])

        pieces = S // PIECE
        h = [keep.tile([P, 2, D, GROUPS * 2], BF16, name=f"h{i}", align_bytes=64) for i in range(pieces)]
        z_codes = [keep.tile([P, GROUPS], U32, name=f"z_codes{i}", align_bytes=64) for i in range(pieces)]
        z_scales = [keep.tile([P, GROUPS], U8, name=f"z_scales{i}", align_bytes=64) for i in range(pieces)]

        def first_layer(i):
            token = i * PIECE
            s = token // SLICE
            cols = slice(token % SLICE, token % SLICE + PIECE)
            for a in range(2):
                bank = hbanks.tile([P, 2, PIECE], F32, name="bank")
                for b in range(2):
                    t = 2 * a + b
                    nc.tensor.matmul_mx(
                        out=bank[:, b, :],
                        lhsT=w1_codes[:, t * P : (t + 1) * P].bitcast(FP8X4),
                        lhsT_scale=w1_scales[:, t * P : (t + 1) * P],
                        rhs=x_codes[s][:, cols].bitcast(FP8X4),
                        rhs_scale=x_scales[s][:, cols],
                        start=True,
                        stop=True,
                    )
                nc.scalar.activation(
                    h[i][:, a].rearrange("p d (v b) -> p d v b", b=2),
                    bank[:].rearrange("p b (v d) -> p d v b", d=D),
                    GELU,
                )

        def pool(i):
            half = keep.tile([P, 2, 2, GROUPS * 2], BF16, name=f"half{i}", align_bytes=64)
            nc.vector.tensor_tensor(
                half[:].rearrange("p a d w -> p a (d w)"),
                h[i][:, :, 0:2].rearrange("p a d w -> p a (d w)"),
                h[i][:, :, 2:4].rearrange("p a d w -> p a (d w)"),
                MAX,
            )
            z = keep.tile([P, GROUPS, 2, 2], BF16, name=f"z{i}", align_bytes=64)
            nc.vector.tensor_tensor(
                z[:],
                half[:, :, 0].rearrange("p a (v b) -> p v a b", b=2),
                half[:, :, 1].rearrange("p a (v b) -> p v a b", b=2),
                MAX,
            )
            nc.vector.quantize_mx(out=z_codes[i][:].bitcast(FP8X4), scales=z_scales[i][:], in_=z[:].rearrange("p v a b -> p (v a b)"))

        def second_layer(i):
            pair = obanks.tile([P, N // P, GROUPS], F32, name="pair")
            for o in range(N // P):
                nc.tensor.matmul_mx(
                    out=pair[:, o, :],
                    lhsT=w2_codes[:, o * P : (o + 1) * P].bitcast(FP8X4),
                    lhsT_scale=w2_scales[:, o * P : (o + 1) * P],
                    rhs=z_codes[i][:].bitcast(FP8X4),
                    rhs_scale=z_scales[i][:],
                    start=True,
                    stop=True,
                )
            result = keep.tile([P, N // P, GROUPS], F32, name=f"result{i}")
            nc.scalar.copy(result[:], pair[:])
            for o in range(N // P):
                nc.vector.tensor_tensor(
                    windows[o][:].indirect(places[:, i * (GROUPS // 16) : (i + 1) * (GROUPS // 16)]),
                    result[:, o, :],
                    gates[:, o, i * GROUPS : (i + 1) * GROUPS],
                    MULT,
                )

        first_layer(0)
        first_layer(1)
        pool(0)
        first_layer(2)
        pool(1)
        second_layer(0)
        first_layer(3)
        pool(2)
        second_layer(1)
        pool(3)
        second_layer(2)
        second_layer(3)
        for o in range(N // P):
            nc.sync.dma_start(out=out[o * P : (o + 1) * P, :], in_=windows[o][:])
